import numpy as np
import ml_dtypes


def mxq(x, axis, fmt="e4m3"):
    dtype, down = {"e4m3": (ml_dtypes.float8_e4m3fn, 7), "e5m2": (ml_dtypes.float8_e5m2, 14)}[fmt]
    v = np.moveaxis(np.asarray(x, np.float32).astype(ml_dtypes.bfloat16).astype(np.float64), axis, -1)
    blocks = v.reshape(v.shape[:-1] + (-1, 32))
    amax = np.abs(blocks).max(-1, keepdims=True)
    byte = np.maximum(np.where(amax > 0, np.frexp(amax)[1] - 1 + 127, 0) - down, 1)
    scale = np.exp2(byte - 127.0)
    codes = (blocks / scale).astype(np.float32).astype(dtype).astype(np.float64)
    return np.moveaxis((codes * scale).reshape(v.shape), -1, axis)


WIDE = False


def mx_kscale(k):
    if not WIDE:
        return np.ones(k)
    levels = np.array([10, -10, 5, -5, 0])
    if k % 512:
        return np.exp2(np.random.permutation(np.resize(levels, k // 32))).repeat(32)
    a = np.empty((k // 512, 16))
    for p in range(k // 512):
        a[p, :8] = np.random.permutation(np.resize(levels, 8))
        for g in range(8):
            far = levels[np.abs(levels - a[p, g]) >= 10]
            a[p, g + 8] = far[np.random.randint(len(far))]
    return np.exp2(a.ravel()).repeat(32)


def f64(x):
    return np.asarray(x).astype(np.float64)


E2M1 = np.array([0.0, 0.5, 1.0, 1.5, 2.0, 3.0, 4.0, 6.0, -0.0, -0.5, -1.0, -1.5, -2.0, -3.0, -4.0, -6.0])


def pack_weight(w, fmt):
    k, n = w.shape
    w = f64(np.asarray(w, np.float32).astype(ml_dtypes.bfloat16)).reshape(k // 32, 32, n)
    amax = np.abs(w).max(1)
    if fmt == "e4m3":
        byte = np.frexp(amax)[1] - 1 + 127 - 7
    else:
        mant, ex = np.frexp(amax / 6.0)
        byte = np.where(mant > 0.5, ex, ex - 1) + 127
    byte = np.clip(np.where(amax > 0, byte, 1), 1, 254)
    scaled = (w * np.exp2(127.0 - byte)[:, None, :]).reshape(k, n).astype(np.float32)
    by_word = np.ascontiguousarray(scaled.reshape(k // 512, 128, 4, n).transpose(0, 1, 3, 2))
    if fmt == "e4m3":
        words = by_word.astype(ml_dtypes.float8_e4m3fn).view(np.uint8)
    else:
        c = by_word.astype(ml_dtypes.float4_e2m1fn).view(np.uint8) & 0xF
        words = (c[..., 0::2] | (c[..., 1::2] << 4)).reshape(k // 512, 128, 2 * n)
    return np.ascontiguousarray(words), np.ascontiguousarray(byte.astype(np.uint8).reshape(k // 512, 16, n))


def unpack_weight(words, scales, fmt):
    g, _, n = scales.shape
    words = np.ascontiguousarray(words).reshape(g, 128, n, -1)
    if fmt == "e4m3":
        vals = words.view(ml_dtypes.float8_e4m3fn).astype(np.float64)
    else:
        nib = np.empty((g, 128, n, 4), np.uint8)
        nib[..., 0::2] = words & 0xF
        nib[..., 1::2] = words >> 4
        vals = E2M1[nib]
    vals = vals * np.repeat(np.exp2(scales.astype(np.float64) - 127.0), 8, axis=1)[..., None]
    return vals.transpose(0, 1, 3, 2).reshape(g * 512, n)


def planes(y):
    n, m = y.shape
    v = y.astype(np.float32).astype(ml_dtypes.bfloat16).astype(np.float64).reshape(n // 32, 32, m)
    top = np.abs(v).max(1)
    byte = np.clip(np.where(top > 0, np.frexp(top)[1] - 1 + 127 - 7, 1), 1, 254)
    codes = (v * np.exp2(127.0 - byte)[:, None, :]).reshape(n, m).astype(np.float32).astype(ml_dtypes.float8_e4m3fn).view(np.uint8)
    words = codes.reshape(n // 512, 128, 4, m).transpose(0, 1, 3, 2)
    return np.ascontiguousarray(words), np.ascontiguousarray(byte.astype(np.uint8).reshape(n // 512, 16, m))


def silu(v):
    return v / (1.0 + np.exp(-np.maximum(v, -700.0)))


K, M, T = 1024, 1536, 512


def setup_inputs():
    n = np.random.standard_normal
    s = mx_kscale(K)[:, None]
    x = n((K, T)) * s
    x4 = pack_weight(x, "e2m1")
    rest = x - unpack_weight(*x4, "e2m1")
    p_w4 = pack_weight(n((K, M)) / np.sqrt(K) / s, "e2m1")
    return {
        "x4_words": x4[0],
        "x4_scales": x4[1],
        "xr": (rest).astype(np.float32),
        "w4_words": p_w4[0],
        "w4_scales": p_w4[1],
        "b": (0.3 * n(1536)).astype(np.float32),
    }


def reference(x4_words, x4_scales, xr, w4_words, w4_scales, b):
    x4_ = unpack_weight(x4_words, x4_scales, "e2m1")
    xr_ = mxq(f64(xr), 0, "e4m3")
    w4_ = unpack_weight(w4_words, w4_scales, "e2m1")
    y = w4_.T @ x4_ + w4_.T @ xr_
    out_0 = silu(y + f64(b)[:, None])
    return (out_0,) + planes(out_0)

@@ -1,0 +1,222 @@
+from contextlib import ExitStack
+
+import concourse.mybir as mybir
+
+K, M, T = 1024, 1536, 512
+FLOPS = 2 * 2 * K * M * T
+
+F32 = mybir.dt.float32
+BF16 = mybir.dt.bfloat16
+I32 = mybir.dt.int32
+U32 = mybir.dt.uint32
+U8 = mybir.dt.uint8
+FP8X4 = mybir.dt.float8_e4m3fn_x4
+FP4X4 = mybir.dt.float4_e2m1fn_x4
+SILU = mybir.ActivationFunctionType.Silu
+
+P = 128
+PACK = 4
+SPAN = P * PACK
+PASSES = K // SPAN
+GROUPS = M // SPAN
+QUADS = 4
+HALF = T // 2
+BANKS = 8
+
+
+def tile_mix_xres_fm_pl_silu_kernel(tc, x4_words, x4_scales, xr, w4_words, w4_scales, b, out_0, out_1, out_2):
+    nc = tc.nc
+    with ExitStack() as ctx:
+        sb = ctx.enter_context(tc.tile_pool(name="sb", bufs=1))
+        psum = ctx.enter_context(tc.psum_pool(name="psum", bufs=1))
+        ctx.enter_context(tc.manual_schedule())
+
+        def sbuf(name, shape, dtype):
+            return sb.tile(shape, dtype, name=name, align_bytes=256)
+
+        w_raw = [sbuf("w_raw%d" % g, [P, PASSES, 2 * SPAN], U8) for g in range(GROUPS)]
+        w_dealt = [[sbuf("w_dealt%d_%d" % (g, a), [P, 2 * SPAN], U8) for a in range(PASSES)] for g in range(GROUPS)]
+        ws_raw = sbuf("ws_raw", [P, PASSES, M], U8)
+        ws_dealt = [sbuf("ws_dealt%d" % g, [P, PASSES, SPAN], U8) for g in range(GROUPS)]
+        x_words = sbuf("x_words", [P, PASSES, 2 * T], U8)
+        x_scales = sbuf("x_scales", [P, PASSES, T], U8)
+        r_raw = [[sbuf("r_raw%d_%d" % (a, h), [P, PACK, HALF], F32) for h in range(2)] for a in range(PASSES)]
+        r_bf = [[sbuf("r_bf%d_%d" % (a, h), [P, HALF, PACK], BF16) for h in range(2)] for a in range(PASSES)]
+        r_words = [sbuf("r_words%d" % a, [P, T], U32) for a in range(PASSES)]
+        r_scales = [sbuf("r_scales%d" % a, [P, T], U8) for a in range(PASSES)]
+        bias = sbuf("bias", [P, GROUPS, PACK], F32)
+        y = [sbuf("y%d" % g, [P, PACK, T], F32) for g in range(GROUPS)]
+        y_bf = [sbuf("y_bf%d" % g, [P, T, PACK], BF16) for g in range(GROUPS)]
+        y_words = [sbuf("y_words%d" % g, [P, T], U32) for g in range(GROUPS)]
+        y_scales = sbuf("y_scales", [P, GROUPS, T], U8)
+        acc = {}
+
+        def load_w(g):
+            src = w4_words[:, :, 2 * SPAN * g : 2 * SPAN * (g + 1)].rearrange("a p c -> p a c")
+            nc.sync.dma_start(out=w_raw[g][:].bitcast(I32), in_=src.bitcast(I32))
+
+        def load_scale_rows(plane, rows, q):
+            src = rows[:, PACK * q : PACK * (q + 1), :].rearrange("a r c -> r a c")
+            nc.sync.dma_start(out=plane[32 * q : 32 * q + PACK, :, :].bitcast(I32), in_=src.bitcast(I32))
+
+        def load_r(a, h):
+            src = xr[SPAN * a : SPAN * (a + 1), HALF * h : HALF * (h + 1)].rearrange("(p i) t -> p i t", i=PACK)
+            nc.sync.dma_start(out=r_raw[a][h][:], in_=src)
+
+        def deal_words(g, a):
+            nc.vector.tensor_copy(
+                out=w_dealt[g][a][:].rearrange("p (r m c) -> p r m c", r=PACK, c=2),
+                in_=w_raw[g][:, a, :].rearrange("p (m r c) -> p r m c", r=PACK, c=2),
+            )
+
+        def deal_scales(g, a0, a1):
+            nc.vector.tensor_copy(
+                out=ws_dealt[g][:, a0:a1, :].rearrange("p a (r m) -> p a r m", r=PACK),
+                in_=ws_raw[:, a0:a1, SPAN * g : SPAN * (g + 1)].rearrange("p a (m r) -> p a r m", r=PACK),
+            )
+
+        def round_r(a, h):
+            src = r_raw[a][h][:].rearrange("p i t -> p t i")
+            if h == 0:
+                nc.scalar.copy(out=r_bf[a][h][:], in_=src)
+            else:
+                nc.vector.tensor_copy(out=r_bf[a][h][:], in_=src)
+
+        def quantise_r(a, h):
+            cols = slice(HALF * h, HALF * (h + 1))
+            nc.vector.quantize_mx(
+                out=r_words[a][:, cols].bitcast(FP8X4),
+                scales=r_scales[a][:, cols],
+                in_=r_bf[a][h][:].rearrange("p t i -> p (t i)"),
+            )
+
+        def multiply(g, r, term, a, start=False, stop=False):
+            if start:
+                bank = (PACK * g + r) % BANKS
+                acc[g, r] = psum.tile([P, T], F32, name="acc%d_%d" % (g, r), tag="bank%d" % bank)
+            if term == "x":
+                rhs, rhs_scale = x_words[:, a, :].bitcast(FP4X4), x_scales[:, a, :]
+            else:
+                rhs, rhs_scale = r_words[a][:].bitcast(FP8X4), r_scales[a][:]
+            nc.tensor.matmul_mx(
+                out=acc[g, r][:],
+                lhsT=w_dealt[g][a][:, 2 * P * r : 2 * P * (r + 1)].bitcast(FP4X4),
+                lhsT_scale=ws_dealt[g][:, a, P * r : P * (r + 1)],
+                rhs=rhs,
+                rhs_scale=rhs_scale,
+                start=start,
+                stop=stop,
+            )
+
+        def activate(g, r, cols=slice(0, T)):
+            nc.scalar.activation(out=y[g][:, r, cols], in_=acc[g, r][:, cols], func=SILU, bias=bias[:, g, r : r + 1])
+
+        def store_y(g, r):
+            dst = out_0[SPAN * g : SPAN * (g + 1), :].rearrange("(p r) t -> p r t", r=PACK)
+            nc.sync.dma_start(out=dst[:, r, :], in_=y[g][:, r, :])
+
+        def round_y(g, cols):
+            nc.vector.tensor_copy(out=y_bf[g][:, cols, :], in_=y[g][:, :, cols].rearrange("p r t -> p t r"))
+
+        def quantise_y(g, cols):
+            nc.vector.quantize_mx(
+                out=y_words[g][:, cols].bitcast(FP8X4),
+                scales=y_scales[:, g, cols],
+                in_=y_bf[g][:, cols, :].rearrange("p t r -> p (t r)"),
+            )
+
+        def store_words(g, cols):
+            dst = out_1[g, :, cols, :].rearrange("p t i -> p (t i)")
+            nc.sync.dma_start(out=dst.bitcast(I32), in_=y_words[g][:, cols].bitcast(I32))
+
+        def store_scales(g0, g1, queues):
+            for q in range(QUADS):
+                dst = out_2[g0:g1, PACK * q : PACK * (q + 1), :].rearrange("a r t -> r a t")
+                queues[q].dma_start(out=dst.bitcast(I32), in_=y_scales[32 * q : 32 * q + PACK, g0:g1, :].bitcast(I32))
+
+        whole = slice(0, T)
+        quarters = [slice(P * c, P * (c + 1)) for c in range(T // P)]
+        halves = [slice(0, HALF), slice(HALF, T)]
+
+        nc.vector.memset(ws_raw[:].bitcast(U32), 0)
+        nc.vector.memset(x_scales[:].bitcast(U32), 0)
+        load_w(0)
+        nc.sync.dma_start(out=x_words[:].bitcast(I32), in_=x4_words.rearrange("a p c -> p a c").bitcast(I32))
+        for q in range(QUADS):
+            load_scale_rows(ws_raw, w4_scales, q)
+        for q in range(QUADS):
+            load_scale_rows(x_scales, x4_scales, q)
+        load_r(0, 0)
+        load_r(0, 1)
+        load_w(1)
+        load_r(1, 0)
+        load_r(1, 1)
+        nc.sync.dma_start(out=bias[:], in_=b.rearrange("(g p r) -> p g r", g=GROUPS, r=PACK))
+        load_w(2)
+
+        deal_words(0, 0)
+        deal_scales(0, 0, 1)
+        deal_words(0, 1)
+        deal_scales(0, 1, 2)
+        deal_scales(1, 0, 2)
+        deal_scales(2, 0, 2)
+        round_r(0, 0)
+        round_r(0, 1)
+        quantise_r(0, 0)
+        quantise_r(0, 1)
+        deal_words(1, 0)
+        deal_words(1, 1)
+        round_r(1, 0)
+        round_r(1, 1)
+        quantise_r(1, 0)
+        quantise_r(1, 1)
+        deal_words(2, 0)
+        deal_words(2, 1)
+
+        for r in range(PACK):
+            multiply(0, r, "x", 0, start=True)
+        for r in range(PACK):
+            multiply(0, r, "x", 1)
+        for r in range(PACK):
+            multiply(0, r, "r", 0)
+        for r in range(PACK):
+            multiply(1, r, "x", 0, start=True)
+        for r in range(PACK):
+            multiply(0, r, "r", 1, stop=True)
+            activate(0, r)
+            store_y(0, r)
+        round_y(0, whole)
+        for r in range(PACK):
+            multiply(1, r, "r", 0)
+            multiply(1, r, "x", 1)
+            multiply(1, r, "r", 1, stop=True)
+            activate(1, r)
+            store_y(1, r)
+            if r == 0:
+                quantise_y(0, whole)
+            if r == 1:
+                store_words(0, whole)
+        round_y(1, whole)
+        for r in range(PACK):
+            multiply(2, r, "x", 0, start=True)
+            multiply(2, r, "r", 0)
+            multiply(2, r, "x", 1)
+            multiply(2, r, "r", 1, stop=True)
+            if r < PACK - 1:
+                activate(2, r)
+            else:
+                for cols in quarters:
+                    activate(2, r, cols)
+            store_y(2, r)
+            if r == 0:
+                quantise_y(1, whole)
+                store_words(1, whole)
+                store_scales(0, 2, [nc.sync] * QUADS)
+        for cols in quarters[:-1]:
+            round_y(2, cols)
+        last = quarters[-1]
+        nc.scalar.copy(out=y_bf[2][:, last, :], in_=y[2][:, :, last].rearrange("p r t -> p t r"))
+        for cols in halves:
+            quantise_y(2, cols)
+            store_words(2, cols)
+        store_scales(2, 3, [nc.scalar, nc.sync, nc.scalar, nc.sync])

@@ -49,15 +49,17 @@ def tile_mix_xres_fm_pl_silu_kernel(tc, x4_words, x4_scales, xr, w4_words, w4_sc
         y_bf = [sbuf("y_bf%d" % g, [P, T, PACK], BF16) for g in range(GROUPS)]
         y_words = [sbuf("y_words%d" % g, [P, T], U32) for g in range(GROUPS)]
         y_scales = sbuf("y_scales", [P, GROUPS, T], U8)
+        warm_in = sbuf("warm_in", [P, 1], F32)
+        warm_out = sbuf("warm_out", [P, 1], F32)
         acc = {}
 
         def load_w(g):
             src = w4_words[:, :, 2 * SPAN * g : 2 * SPAN * (g + 1)].rearrange("a p c -> p a c")
             nc.sync.dma_start(out=w_raw[g][:].bitcast(I32), in_=src.bitcast(I32))
 
-        def load_scale_rows(plane, rows, q):
+        def load_scale_rows(queue, plane, rows, q):
             src = rows[:, PACK * q : PACK * (q + 1), :].rearrange("a r c -> r a c")
-            nc.sync.dma_start(out=plane[32 * q : 32 * q + PACK, :, :].bitcast(I32), in_=src.bitcast(I32))
+            queue.dma_start(out=plane[32 * q : 32 * q + PACK, :, :].bitcast(I32), in_=src.bitcast(I32))
 
         def load_r(a, h):
             src = xr[SPAN * a : SPAN * (a + 1), HALF * h : HALF * (h + 1)].rearrange("(p i) t -> p i t", i=PACK)
@@ -75,12 +77,12 @@ def tile_mix_xres_fm_pl_silu_kernel(tc, x4_words, x4_scales, xr, w4_words, w4_sc
                 in_=ws_raw[:, a0:a1, SPAN * g : SPAN * (g + 1)].rearrange("p a (m r) -> p a r m", r=PACK),
             )
 
-        def round_r(a, h):
-            src = r_raw[a][h][:].rearrange("p i t -> p t i")
-            if h == 0:
-                nc.scalar.copy(out=r_bf[a][h][:], in_=src)
-            else:
-                nc.vector.tensor_copy(out=r_bf[a][h][:], in_=src)
+        def interleaved(dst, src):
+            return dst.rearrange("p (c u) i -> p c i u", u=4), src.rearrange("p i (c u) -> p c i u", u=4)
+
+        def round_r(a, h, copy):
+            dst, src = interleaved(r_bf[a][h][:], r_raw[a][h][:])
+            copy(out=dst, in_=src)
 
         def quantise_r(a, h):
             cols = slice(HALF * h, HALF * (h + 1))
@@ -116,7 +118,8 @@ def tile_mix_xres_fm_pl_silu_kernel(tc, x4_words, x4_scales, xr, w4_words, w4_sc
             nc.sync.dma_start(out=dst[:, r, :], in_=y[g][:, r, :])
 
         def round_y(g, cols):
-            nc.vector.tensor_copy(out=y_bf[g][:, cols, :], in_=y[g][:, :, cols].rearrange("p r t -> p t r"))
+            dst, src = interleaved(y_bf[g][:, cols, :], y[g][:, :, cols])
+            nc.vector.tensor_copy(out=dst, in_=src)
 
         def quantise_y(g, cols):
             nc.vector.quantize_mx(
@@ -138,56 +141,59 @@ def tile_mix_xres_fm_pl_silu_kernel(tc, x4_words, x4_scales, xr, w4_words, w4_sc
         quarters = [slice(P * c, P * (c + 1)) for c in range(T // P)]
         halves = [slice(0, HALF), slice(HALF, T)]
 
-        nc.vector.memset(ws_raw[:].bitcast(U32), 0)
         nc.vector.memset(x_scales[:].bitcast(U32), 0)
+        nc.vector.memset(ws_raw[:].bitcast(U32), 0)
+        for q in range(2):
+            load_scale_rows(nc.sync, x_scales, x4_scales, q)
         load_w(0)
         nc.sync.dma_start(out=x_words[:].bitcast(I32), in_=x4_words.rearrange("a p c -> p a c").bitcast(I32))
         for q in range(QUADS):
-            load_scale_rows(ws_raw, w4_scales, q)
-        for q in range(QUADS):
-            load_scale_rows(x_scales, x4_scales, q)
+            load_scale_rows(nc.sync, ws_raw, w4_scales, q)
+        for q in range(2, QUADS):
+            load_scale_rows(nc.sync, x_scales, x4_scales, q)
         load_r(0, 0)
-        load_r(0, 1)
         load_w(1)
+        load_r(0, 1)
         load_r(1, 0)
         load_r(1, 1)
         nc.sync.dma_start(out=bias[:], in_=b.rearrange("(g p r) -> p g r", g=GROUPS, r=PACK))
         load_w(2)
 
+        nc.gpsimd.memset(warm_in[:], 0.0)
+        nc.scalar.activation(out=warm_out[:], in_=warm_in[:], func=SILU)
+        round_r(0, 0, nc.scalar.copy)
+        round_r(0, 1, nc.scalar.copy)
+        round_r(1, 0, nc.scalar.copy)
         deal_words(0, 0)
         deal_scales(0, 0, 1)
         deal_words(0, 1)
         deal_scales(0, 1, 2)
-        deal_scales(1, 0, 2)
-        deal_scales(2, 0, 2)
-        round_r(0, 0)
-        round_r(0, 1)
+        deal_scales(1, 0, 1)
+        deal_words(1, 0)
         quantise_r(0, 0)
         quantise_r(0, 1)
-        deal_words(1, 0)
-        deal_words(1, 1)
-        round_r(1, 0)
-        round_r(1, 1)
+        deal_scales(1, 1, 2)
+        round_r(1, 1, nc.vector.tensor_copy)
         quantise_r(1, 0)
         quantise_r(1, 1)
+        deal_words(1, 1)
+        deal_scales(2, 0, 2)
         deal_words(2, 0)
         deal_words(2, 1)
 
-        for r in range(PACK):
-            multiply(0, r, "x", 0, start=True)
-        for r in range(PACK):
-            multiply(0, r, "x", 1)
-        for r in range(PACK):
-            multiply(0, r, "r", 0)
-        for r in range(PACK):
-            multiply(1, r, "x", 0, start=True)
+        for g, term, a in ((0, "x", 0), (0, "x", 1), (1, "x", 0), (0, "r", 0)):
+            for r in range(PACK):
+                multiply(g, r, term, a, start=(term == "x" and a == 0))
+        for r in range(2):
+            multiply(1, r, "r", 0)
         for r in range(PACK):
             multiply(0, r, "r", 1, stop=True)
             activate(0, r)
             store_y(0, r)
         round_y(0, whole)
         for r in range(PACK):
-            multiply(1, r, "r", 0)
+            if r >= 2:
+                multiply(1, r, "r", 0)
             multiply(1, r, "x", 1)
             multiply(1, r, "r", 1, stop=True)
             activate(1, r)
@@ -211,12 +217,12 @@ def tile_mix_xres_fm_pl_silu_kernel(tc, x4_words, x4_scales, xr, w4_words, w4_sc
             if r == 0:
                 quantise_y(1, whole)
                 store_words(1, whole)
-                store_scales(0, 2, [nc.sync] * QUADS)
         for cols in quarters[:-1]:
             round_y(2, cols)
         last = quarters[-1]
-        nc.scalar.copy(out=y_bf[2][:, last, :], in_=y[2][:, :, last].rearrange("p r t -> p t r"))
+        dst, src = interleaved(y_bf[2][:, last, :], y[2][:, :, last])
+        nc.scalar.copy(out=dst, in_=src)
         for cols in halves:
             quantise_y(2, cols)
             store_words(2, cols)
-        store_scales(2, 3, [nc.scalar, nc.sync, nc.scalar, nc.sync])
+        store_scales(0, GROUPS, [nc.scalar, nc.sync, nc.scalar, nc.sync])

@@ -22,6 +22,8 @@ GROUPS = M // SPAN
 QUADS = 4
 HALF = T // 2
 BANKS = 8
+SPLIT = 320
+FILL = 3
 
 
 def tile_mix_xres_fm_pl_silu_kernel(tc, x4_words, x4_scales, xr, w4_words, w4_scales, b, out_0, out_1, out_2):
@@ -34,14 +36,14 @@ def tile_mix_xres_fm_pl_silu_kernel(tc, x4_words, x4_scales, xr, w4_words, w4_sc
         def sbuf(name, shape, dtype):
             return sb.tile(shape, dtype, name=name, align_bytes=256)
 
-        w_raw = [sbuf("w_raw%d" % g, [P, PASSES, 2 * SPAN], U8) for g in range(GROUPS)]
+        w_raw = sbuf("w_raw", [P, PASSES, 2 * M], U8)
         w_dealt = [[sbuf("w_dealt%d_%d" % (g, a), [P, 2 * SPAN], U8) for a in range(PASSES)] for g in range(GROUPS)]
         ws_raw = sbuf("ws_raw", [P, PASSES, M], U8)
         ws_dealt = [sbuf("ws_dealt%d" % g, [P, PASSES, SPAN], U8) for g in range(GROUPS)]
         x_words = sbuf("x_words", [P, PASSES, 2 * T], U8)
         x_scales = sbuf("x_scales", [P, PASSES, T], U8)
-        r_raw = [[sbuf("r_raw%d_%d" % (a, h), [P, PACK, HALF], F32) for h in range(2)] for a in range(PASSES)]
-        r_bf = [[sbuf("r_bf%d_%d" % (a, h), [P, HALF, PACK], BF16) for h in range(2)] for a in range(PASSES)]
+        r_raw = [sbuf("r_raw%d" % a, [P, PACK, T], F32) for a in range(PASSES)]
+        r_bf = [sbuf("r_bf%d" % a, [P, T, PACK], BF16) for a in range(PASSES)]
         r_words = [sbuf("r_words%d" % a, [P, T], U32) for a in range(PASSES)]
         r_scales = [sbuf("r_scales%d" % a, [P, T], U8) for a in range(PASSES)]
         bias = sbuf("bias", [P, GROUPS, PACK], F32)
@@ -53,22 +55,23 @@ def tile_mix_xres_fm_pl_silu_kernel(tc, x4_words, x4_scales, xr, w4_words, w4_sc
         warm_out = sbuf("warm_out", [P, 1], F32)
         acc = {}
 
-        def load_w(g):
-            src = w4_words[:, :, 2 * SPAN * g : 2 * SPAN * (g + 1)].rearrange("a p c -> p a c")
-            nc.sync.dma_start(out=w_raw[g][:].bitcast(I32), in_=src.bitcast(I32))
+        def load_w(a, g0, g1):
+            cols = slice(2 * SPAN * g0, 2 * SPAN * g1)
+            nc.sync.dma_start(out=w_raw[:, a, cols].bitcast(I32), in_=w4_words[a, :, cols].bitcast(I32))
 
-        def load_scale_rows(queue, plane, rows, q):
-            src = rows[:, PACK * q : PACK * (q + 1), :].rearrange("a r c -> r a c")
-            queue.dma_start(out=plane[32 * q : 32 * q + PACK, :, :].bitcast(I32), in_=src.bitcast(I32))
+        def load_scale_rows(plane, rows, j):
+            src = rows.rearrange("a (q j) c -> j q a c", j=PACK)[j]
+            nc.sync.dma_start(out=plane[j:P:32, :, :].bitcast(I32), in_=src.bitcast(I32))
 
-        def load_r(a, h):
-            src = xr[SPAN * a : SPAN * (a + 1), HALF * h : HALF * (h + 1)].rearrange("(p i) t -> p i t", i=PACK)
-            nc.sync.dma_start(out=r_raw[a][h][:], in_=src)
+        def load_r(a):
+            src = xr[SPAN * a : SPAN * (a + 1), :].rearrange("(p i) t -> p i t", i=PACK)
+            nc.sync.dma_start(out=r_raw[a][:], in_=src)
 
         def deal_words(g, a):
+            raw = w_raw[:, a, 2 * SPAN * g : 2 * SPAN * (g + 1)]
             nc.vector.tensor_copy(
                 out=w_dealt[g][a][:].rearrange("p (r m c) -> p r m c", r=PACK, c=2),
-                in_=w_raw[g][:, a, :].rearrange("p (m r c) -> p r m c", r=PACK, c=2),
+                in_=raw.rearrange("p (m r c) -> p r m c", r=PACK, c=2),
             )
 
         def deal_scales(g, a0, a1):
@@ -80,8 +83,8 @@ def tile_mix_xres_fm_pl_silu_kernel(tc, x4_words, x4_scales, xr, w4_words, w4_sc
         def interleaved(dst, src):
             return dst.rearrange("p (c u) i -> p c i u", u=4), src.rearrange("p i (c u) -> p c i u", u=4)
 
-        def round_r(a, h, copy):
-            dst, src = interleaved(r_bf[a][h][:], r_raw[a][h][:])
+        def round_r(a, cols, copy):
+            dst, src = interleaved(r_bf[a][:, cols, :], r_raw[a][:, :, cols])
             copy(out=dst, in_=src)
 
         def quantise_r(a, h):
@@ -89,19 +92,21 @@ def tile_mix_xres_fm_pl_silu_kernel(tc, x4_words, x4_scales, xr, w4_words, w4_sc
             nc.vector.quantize_mx(
                 out=r_words[a][:, cols].bitcast(FP8X4),
                 scales=r_scales[a][:, cols],
-                in_=r_bf[a][h][:].rearrange("p t i -> p (t i)"),
+                in_=r_bf[a][:, cols, :].rearrange("p t i -> p (t i)"),
             )
 
-        def multiply(g, r, term, a, start=False, stop=False):
+        def multiply(g, r, term, a, cols, start=False, stop=False):
             if start:
-                bank = (PACK * g + r) % BANKS
-                acc[g, r] = psum.tile([P, T], F32, name="acc%d_%d" % (g, r), tag="bank%d" % bank)
+                bank = len(acc) % BANKS
+                acc[g, r, cols.start] = psum.tile([P, cols.stop - cols.start], F32, name="acc%d" % len(acc), tag="bank%d" % bank)
             if term == "x":
-                rhs, rhs_scale = x_words[:, a, :].bitcast(FP4X4), x_scales[:, a, :]
+                rhs = x_words[:, a, 2 * cols.start : 2 * cols.stop].bitcast(FP4X4)
+                rhs_scale = x_scales[:, a, cols]
             else:
-                rhs, rhs_scale = r_words[a][:].bitcast(FP8X4), r_scales[a][:]
+                rhs = r_words[a][:, cols].bitcast(FP8X4)
+                rhs_scale = r_scales[a][:, cols]
             nc.tensor.matmul_mx(
-                out=acc[g, r][:],
+                out=acc[g, r, cols.start][:],
                 lhsT=w_dealt[g][a][:, 2 * P * r : 2 * P * (r + 1)].bitcast(FP4X4),
                 lhsT_scale=ws_dealt[g][:, a, P * r : P * (r + 1)],
                 rhs=rhs,
@@ -110,12 +115,12 @@ def tile_mix_xres_fm_pl_silu_kernel(tc, x4_words, x4_scales, xr, w4_words, w4_sc
                 stop=stop,
             )
 
-        def activate(g, r, cols=slice(0, T)):
-            nc.scalar.activation(out=y[g][:, r, cols], in_=acc[g, r][:, cols], func=SILU, bias=bias[:, g, r : r + 1])
+        def activate(g, r, cols):
+            nc.scalar.activation(out=y[g][:, r, cols], in_=acc[g, r, cols.start][:], func=SILU, bias=bias[:, g, r : r + 1])
 
-        def store_y(g, r):
+        def store_y(g, r0, r1):
             dst = out_0[SPAN * g : SPAN * (g + 1), :].rearrange("(p r) t -> p r t", r=PACK)
-            nc.sync.dma_start(out=dst[:, r, :], in_=y[g][:, r, :])
+            nc.sync.dma_start(out=dst[:, r0:r1, :], in_=y[g][:, r0:r1, :])
 
         def round_y(g, cols):
             dst, src = interleaved(y_bf[g][:, cols, :], y[g][:, :, cols])
@@ -132,10 +137,10 @@ def tile_mix_xres_fm_pl_silu_kernel(tc, x4_words, x4_scales, xr, w4_words, w4_sc
             dst = out_1[g, :, cols, :].rearrange("p t i -> p (t i)")
             nc.sync.dma_start(out=dst.bitcast(I32), in_=y_words[g][:, cols].bitcast(I32))
 
-        def store_scales(g0, g1, queues):
-            for q in range(QUADS):
-                dst = out_2[g0:g1, PACK * q : PACK * (q + 1), :].rearrange("a r t -> r a t")
-                queues[q].dma_start(out=dst.bitcast(I32), in_=y_scales[32 * q : 32 * q + PACK, g0:g1, :].bitcast(I32))
+        def store_scales(queues):
+            for j in range(PACK):
+                dst = out_2.rearrange("a (q j) t -> j q a t", j=PACK)[j]
+                queues[j].dma_start(out=dst.bitcast(I32), in_=y_scales[j:P:32, :, :].bitcast(I32))
 
         whole = slice(0, T)
         quarters = [slice(P * c, P * (c + 1)) for c in range(T // P)]
@@ -143,86 +148,94 @@ def tile_mix_xres_fm_pl_silu_kernel(tc, x4_words, x4_scales, xr, w4_words, w4_sc
 
         nc.vector.memset(x_scales[:].bitcast(U32), 0)
         nc.vector.memset(ws_raw[:].bitcast(U32), 0)
-        for q in range(2):
-            load_scale_rows(nc.sync, x_scales, x4_scales, q)
-        load_w(0)
+        for j in range(2):
+            load_scale_rows(x_scales, x4_scales, j)
+        load_w(0, 0, 1)
         nc.sync.dma_start(out=x_words[:].bitcast(I32), in_=x4_words.rearrange("a p c -> p a c").bitcast(I32))
-        for q in range(QUADS):
-            load_scale_rows(nc.sync, ws_raw, w4_scales, q)
-        for q in range(2, QUADS):
-            load_scale_rows(nc.sync, x_scales, x4_scales, q)
-        load_r(0, 0)
-        load_w(1)
-        load_r(0, 1)
-        load_r(1, 0)
-        load_r(1, 1)
+        for j in range(PACK):
+            load_scale_rows(ws_raw, w4_scales, j)
+        for j in range(2, PACK):
+            load_scale_rows(x_scales, x4_scales, j)
+        load_w(1, 0, 2)
+        load_r(0)
+        load_w(0, 1, 2)
+        load_r(1)
         nc.sync.dma_start(out=bias[:], in_=b.rearrange("(g p r) -> p g r", g=GROUPS, r=PACK))
-        load_w(2)
+        load_w(0, 2, 3)
+        load_w(1, 2, 3)
 
         nc.gpsimd.memset(warm_in[:], 0.0)
         nc.scalar.activation(out=warm_out[:], in_=warm_in[:], func=SILU)
-        round_r(0, 0, nc.scalar.copy)
-        round_r(0, 1, nc.scalar.copy)
-        round_r(1, 0, nc.scalar.copy)
+        round_r(0, halves[1], nc.scalar.copy)
+        round_r(1, slice(SPLIT, T), nc.scalar.copy)
         deal_words(0, 0)
         deal_scales(0, 0, 1)
         deal_words(0, 1)
         deal_scales(0, 1, 2)
+        deal_words(1, 1)
+        deal_scales(1, 1, 2)
+        round_r(0, halves[0], nc.vector.tensor_copy)
         deal_scales(1, 0, 1)
-        deal_words(1, 0)
         quantise_r(0, 0)
         quantise_r(0, 1)
-        deal_scales(1, 1, 2)
-        round_r(1, 1, nc.vector.tensor_copy)
+        deal_words(1, 0)
+        round_r(1, halves[0], nc.vector.tensor_copy)
+        round_r(1, slice(HALF, SPLIT), nc.vector.tensor_copy)
         quantise_r(1, 0)
         quantise_r(1, 1)
-        deal_words(1, 1)
         deal_scales(2, 0, 2)
         deal_words(2, 0)
         deal_words(2, 1)
 
-        for g, term, a in ((0, "x", 0), (0, "x", 1), (1, "x", 0), (0, "r", 0)):
-            for r in range(PACK):
-                multiply(g, r, term, a, start=(term == "x" and a == 0))
-        for r in range(2):
-            multiply(1, r, "r", 0)
         for r in range(PACK):
-            multiply(0, r, "r", 1, stop=True)
-            activate(0, r)
-            store_y(0, r)
+            multiply(0, r, "x", 0, whole, start=True)
+        for r in range(PACK):
+            multiply(0, r, "x", 1, whole)
+        for r in range(PACK):
+            multiply(1, r, "x", 1, whole, start=True)
+        for r in range(PACK):
+            multiply(0, r, "r", 0, whole)
+        for r in range(FILL):
+            multiply(1, r, "x", 0, whole)
+        for r in range(PACK):
+            multiply(0, r, "r", 1, whole, stop=True)
+            activate(0, r, whole)
+            if r != 2:
+                store_y(0, min(r, 2), r + 1)
         round_y(0, whole)
         for r in range(PACK):
-            if r >= 2:
-                multiply(1, r, "r", 0)
-            multiply(1, r, "x", 1)
-            multiply(1, r, "r", 1, stop=True)
-            activate(1, r)
-            store_y(1, r)
+            if r >= FILL:
+                multiply(1, r, "x", 0, whole)
+            multiply(1, r, "r", 0, whole)
+            multiply(1, r, "r", 1, whole, stop=True)
+            activate(1, r, whole)
             if r == 0:
                 quantise_y(0, whole)
+            if r % 2 == 1:
+                store_y(1, r - 1, r + 1)
             if r == 1:
                 store_words(0, whole)
         round_y(1, whole)
+        quantise_y(1, whole)
         for r in range(PACK):
-            multiply(2, r, "x", 0, start=True)
-            multiply(2, r, "r", 0)
-            multiply(2, r, "x", 1)
-            multiply(2, r, "r", 1, stop=True)
-            if r < PACK - 1:
-                activate(2, r)
-            else:
-                for cols in quarters:
-                    activate(2, r, cols)
-            store_y(2, r)
+            for cols in [whole] if r < PACK - 1 else quarters:
+                multiply(2, r, "x", 0, cols, start=True)
+                multiply(2, r, "r", 0, cols)
+                multiply(2, r, "x", 1, cols)
+                multiply(2, r, "r", 1, cols, stop=True)
+                activate(2, r, cols)
             if r == 0:
-                quantise_y(1, whole)
                 store_words(1, whole)
-        for cols in quarters[:-1]:
-            round_y(2, cols)
-        last = quarters[-1]
-        dst, src = interleaved(y_bf[2][:, last, :], y[2][:, :, last])
-        nc.scalar.copy(out=dst, in_=src)
-        for cols in halves:
-            quantise_y(2, cols)
-            store_words(2, cols)
-        store_scales(0, GROUPS, [nc.scalar, nc.sync, nc.scalar, nc.sync])
+            else:
+                store_y(2, 0 if r == 1 else r, r + 1)
+        round_y(2, quarters[0])
+        round_y(2, quarters[1])
+        quantise_y(2, quarters[0])
+        round_y(2, quarters[2])
+        quantise_y(2, quarters[1])
+        store_words(2, halves[0])
+        round_y(2, quarters[3])
+        quantise_y(2, quarters[2])
+        quantise_y(2, quarters[3])
+        store_words(2, halves[1])
+        store_scales([nc.scalar, nc.sync, nc.scalar, nc.sync])

@@ -23,7 +23,6 @@ QUADS = 4
 HALF = T // 2
 BANKS = 8
 SPLIT = 320
-FILL = 3
 
 
 def tile_mix_xres_fm_pl_silu_kernel(tc, x4_words, x4_scales, xr, w4_words, w4_scales, b, out_0, out_1, out_2):
@@ -118,9 +117,9 @@ def tile_mix_xres_fm_pl_silu_kernel(tc, x4_words, x4_scales, xr, w4_words, w4_sc
         def activate(g, r, cols):
             nc.scalar.activation(out=y[g][:, r, cols], in_=acc[g, r, cols.start][:], func=SILU, bias=bias[:, g, r : r + 1])
 
-        def store_y(g, r0, r1):
+        def store_y(g, r0, r1, cols):
             dst = out_0[SPAN * g : SPAN * (g + 1), :].rearrange("(p r) t -> p r t", r=PACK)
-            nc.sync.dma_start(out=dst[:, r0:r1, :], in_=y[g][:, r0:r1, :])
+            nc.sync.dma_start(out=dst[:, r0:r1, cols], in_=y[g][:, r0:r1, cols])
 
         def round_y(g, cols):
             dst, src = interleaved(y_bf[g][:, cols, :], y[g][:, :, cols])
@@ -137,10 +136,10 @@ def tile_mix_xres_fm_pl_silu_kernel(tc, x4_words, x4_scales, xr, w4_words, w4_sc
             dst = out_1[g, :, cols, :].rearrange("p t i -> p (t i)")
             nc.sync.dma_start(out=dst.bitcast(I32), in_=y_words[g][:, cols].bitcast(I32))
 
-        def store_scales(queues):
+        def store_scales(g0, g1, queues):
             for j in range(PACK):
-                dst = out_2.rearrange("a (q j) t -> j q a t", j=PACK)[j]
-                queues[j].dma_start(out=dst.bitcast(I32), in_=y_scales[j:P:32, :, :].bitcast(I32))
+                dst = out_2[g0:g1].rearrange("a (q j) t -> j q a t", j=PACK)[j]
+                queues[j].dma_start(out=dst.bitcast(I32), in_=y_scales[j:P:32, g0:g1, :].bitcast(I32))
 
         whole = slice(0, T)
         quarters = [slice(P * c, P * (c + 1)) for c in range(T // P)]
@@ -148,9 +147,9 @@ def tile_mix_xres_fm_pl_silu_kernel(tc, x4_words, x4_scales, xr, w4_words, w4_sc
 
         nc.vector.memset(x_scales[:].bitcast(U32), 0)
         nc.vector.memset(ws_raw[:].bitcast(U32), 0)
+        load_w(0, 0, 1)
         for j in range(2):
             load_scale_rows(x_scales, x4_scales, j)
-        load_w(0, 0, 1)
         nc.sync.dma_start(out=x_words[:].bitcast(I32), in_=x4_words.rearrange("a p c -> p a c").bitcast(I32))
         for j in range(PACK):
             load_scale_rows(ws_raw, w4_scales, j)
@@ -166,6 +165,7 @@ def tile_mix_xres_fm_pl_silu_kernel(tc, x4_words, x4_scales, xr, w4_words, w4_sc
 
         nc.gpsimd.memset(warm_in[:], 0.0)
         nc.scalar.activation(out=warm_out[:], in_=warm_in[:], func=SILU)
+        round_r(0, quarters[1], nc.scalar.copy)
         round_r(0, halves[1], nc.scalar.copy)
         round_r(1, slice(SPLIT, T), nc.scalar.copy)
         deal_words(0, 0)
@@ -174,11 +174,11 @@ def tile_mix_xres_fm_pl_silu_kernel(tc, x4_words, x4_scales, xr, w4_words, w4_sc
         deal_scales(0, 1, 2)
         deal_words(1, 1)
         deal_scales(1, 1, 2)
-        round_r(0, halves[0], nc.vector.tensor_copy)
         deal_scales(1, 0, 1)
+        round_r(0, quarters[0], nc.vector.tensor_copy)
+        deal_words(1, 0)
         quantise_r(0, 0)
         quantise_r(0, 1)
-        deal_words(1, 0)
         round_r(1, halves[0], nc.vector.tensor_copy)
         round_r(1, slice(HALF, SPLIT), nc.vector.tensor_copy)
         quantise_r(1, 0)
@@ -193,26 +193,25 @@ def tile_mix_xres_fm_pl_silu_kernel(tc, x4_words, x4_scales, xr, w4_words, w4_sc
             multiply(0, r, "x", 1, whole)
         for r in range(PACK):
             multiply(1, r, "x", 1, whole, start=True)
+        for r in range(PACK - 1):
+            multiply(1, r, "x", 0, whole)
         for r in range(PACK):
             multiply(0, r, "r", 0, whole)
-        for r in range(FILL):
-            multiply(1, r, "x", 0, whole)
         for r in range(PACK):
             multiply(0, r, "r", 1, whole, stop=True)
             activate(0, r, whole)
-            if r != 2:
-                store_y(0, min(r, 2), r + 1)
+            store_y(0, r, r + 1, whole)
         round_y(0, whole)
         for r in range(PACK):
-            if r >= FILL:
+            if r == PACK - 1:
                 multiply(1, r, "x", 0, whole)
             multiply(1, r, "r", 0, whole)
             multiply(1, r, "r", 1, whole, stop=True)
             activate(1, r, whole)
             if r == 0:
                 quantise_y(0, whole)
-            if r % 2 == 1:
-                store_y(1, r - 1, r + 1)
+            if r != 2:
+                store_y(1, min(r, 2), r + 1, whole)
             if r == 1:
                 store_words(0, whole)
         round_y(1, whole)
@@ -224,18 +223,21 @@ def tile_mix_xres_fm_pl_silu_kernel(tc, x4_words, x4_scales, xr, w4_words, w4_sc
                 multiply(2, r, "x", 1, cols)
                 multiply(2, r, "r", 1, cols, stop=True)
                 activate(2, r, cols)
-            if r == 0:
+            if r == 1:
+                store_y(2, 0, 2, whole)
                 store_words(1, whole)
-            else:
-                store_y(2, 0 if r == 1 else r, r + 1)
+            elif r == 2:
+                store_y(2, 2, 3, whole)
+        store_y(2, 3, 4, whole)
         round_y(2, quarters[0])
         round_y(2, quarters[1])
         quantise_y(2, quarters[0])
         round_y(2, quarters[2])
         quantise_y(2, quarters[1])
         store_words(2, halves[0])
-        round_y(2, quarters[3])
+        dst, src = interleaved(y_bf[2][:, quarters[3], :], y[2][:, :, quarters[3]])
+        nc.scalar.copy(out=dst, in_=src)
         quantise_y(2, quarters[2])
         quantise_y(2, quarters[3])
         store_words(2, halves[1])
-        store_scales([nc.scalar, nc.sync, nc.scalar, nc.sync])
+        store_scales(0, 3, [nc.scalar, nc.sync, nc.scalar, nc.sync])

@@ -37,7 +37,8 @@ def tile_mix_xres_fm_pl_silu_kernel(tc, x4_words, x4_scales, xr, w4_words, w4_sc
 
         w_raw = sbuf("w_raw", [P, PASSES, 2 * M], U8)
         w_dealt = [[sbuf("w_dealt%d_%d" % (g, a), [P, 2 * SPAN], U8) for a in range(PASSES)] for g in range(GROUPS)]
-        ws_raw = sbuf("ws_raw", [P, PASSES, M], U8)
+        ws_early = sbuf("ws_early", [P, PASSES, 2 * SPAN], U8)
+        ws_late = sbuf("ws_late", [P, PASSES, SPAN], U8)
         ws_dealt = [sbuf("ws_dealt%d" % g, [P, PASSES, SPAN], U8) for g in range(GROUPS)]
         x_words = sbuf("x_words", [P, PASSES, 2 * T], U8)
         x_scales = sbuf("x_scales", [P, PASSES, T], U8)
@@ -74,9 +75,10 @@ def tile_mix_xres_fm_pl_silu_kernel(tc, x4_words, x4_scales, xr, w4_words, w4_sc
             )
 
         def deal_scales(g, a0, a1):
+            raw = ws_early[:, a0:a1, SPAN * g : SPAN * (g + 1)] if g < 2 else ws_late[:, a0:a1, :]
             nc.vector.tensor_copy(
                 out=ws_dealt[g][:, a0:a1, :].rearrange("p a (r m) -> p a r m", r=PACK),
-                in_=ws_raw[:, a0:a1, SPAN * g : SPAN * (g + 1)].rearrange("p a (m r) -> p a r m", r=PACK),
+                in_=raw.rearrange("p a (m r) -> p a r m", r=PACK),
             )
 
         def interleaved(dst, src):
@@ -146,13 +148,14 @@ def tile_mix_xres_fm_pl_silu_kernel(tc, x4_words, x4_scales, xr, w4_words, w4_sc
         halves = [slice(0, HALF), slice(HALF, T)]
 
         nc.vector.memset(x_scales[:].bitcast(U32), 0)
-        nc.vector.memset(ws_raw[:].bitcast(U32), 0)
+        nc.vector.memset(ws_early[:].bitcast(U32), 0)
+        nc.vector.memset(ws_late[:].bitcast(U32), 0)
         load_w(0, 0, 1)
         for j in range(2):
             load_scale_rows(x_scales, x4_scales, j)
-        nc.sync.dma_start(out=x_words[:].bitcast(I32), in_=x4_words.rearrange("a p c -> p a c").bitcast(I32))
         for j in range(PACK):
-            load_scale_rows(ws_raw, w4_scales, j)
+            load_scale_rows(ws_early, w4_scales[:, :, 0 : 2 * SPAN], j)
+        nc.sync.dma_start(out=x_words[:].bitcast(I32), in_=x4_words.rearrange("a p c -> p a c").bitcast(I32))
         for j in range(2, PACK):
             load_scale_rows(x_scales, x4_scales, j)
         load_w(1, 0, 2)
@@ -160,6 +163,8 @@ def tile_mix_xres_fm_pl_silu_kernel(tc, x4_words, x4_scales, xr, w4_words, w4_sc
         load_w(0, 1, 2)
         load_r(1)
         nc.sync.dma_start(out=bias[:], in_=b.rearrange("(g p r) -> p g r", g=GROUPS, r=PACK))
+        for j in range(PACK):
+            load_scale_rows(ws_late, w4_scales[:, :, 2 * SPAN : 3 * SPAN], j)
         load_w(0, 2, 3)
         load_w(1, 2, 3)
 

from contextlib import ExitStack

import concourse.mybir as mybir

K, M, T = 1024, 1536, 512
FLOPS = 2 * 2 * K * M * T

F32 = mybir.dt.float32
BF16 = mybir.dt.bfloat16
I32 = mybir.dt.int32
U32 = mybir.dt.uint32
U8 = mybir.dt.uint8
FP8X4 = mybir.dt.float8_e4m3fn_x4
FP4X4 = mybir.dt.float4_e2m1fn_x4
SILU = mybir.ActivationFunctionType.Silu

P = 128
PACK = 4
SPAN = P * PACK
PASSES = K // SPAN
GROUPS = M // SPAN
QUADS = 4
HALF = T // 2
BANKS = 8
SPLIT = 320


def tile_mix_xres_fm_pl_silu_kernel(tc, x4_words, x4_scales, xr, w4_words, w4_scales, b, out_0, out_1, out_2):
    nc = tc.nc
    with ExitStack() as ctx:
        sb = ctx.enter_context(tc.tile_pool(name="sb", bufs=1))
        psum = ctx.enter_context(tc.psum_pool(name="psum", bufs=1))
        ctx.enter_context(tc.manual_schedule())

        def sbuf(name, shape, dtype):
            return sb.tile(shape, dtype, name=name, align_bytes=256)

        w_raw = sbuf("w_raw", [P, PASSES, 2 * M], U8)
        w_dealt = [[sbuf("w_dealt%d_%d" % (g, a), [P, 2 * SPAN], U8) for a in range(PASSES)] for g in range(GROUPS)]
        ws_early = sbuf("ws_early", [P, PASSES, 2 * SPAN], U8)
        ws_late = sbuf("ws_late", [P, PASSES, SPAN], U8)
        ws_dealt = [sbuf("ws_dealt%d" % g, [P, PASSES, SPAN], U8) for g in range(GROUPS)]
        x_words = sbuf("x_words", [P, PASSES, 2 * T], U8)
        x_scales = sbuf("x_scales", [P, PASSES, T], U8)
        r_raw = [sbuf("r_raw%d" % a, [P, PACK, T], F32) for a in range(PASSES)]
        r_bf = [sbuf("r_bf%d" % a, [P, T, PACK], BF16) for a in range(PASSES)]
        r_words = [sbuf("r_words%d" % a, [P, T], U32) for a in range(PASSES)]
        r_scales = [sbuf("r_scales%d" % a, [P, T], U8) for a in range(PASSES)]
        bias = sbuf("bias", [P, GROUPS, PACK], F32)
        y = [sbuf("y%d" % g, [P, PACK, T], F32) for g in range(GROUPS)]
        y_bf = [sbuf("y_bf%d" % g, [P, T, PACK], BF16) for g in range(GROUPS)]
        y_words = [sbuf("y_words%d" % g, [P, T], U32) for g in range(GROUPS)]
        y_scales = sbuf("y_scales", [P, GROUPS, T], U8)
        warm_in = sbuf("warm_in", [P, 1], F32)
        warm_out = sbuf("warm_out", [P, 1], F32)
        acc = {}

        def load_w(a, g0, g1):
            cols = slice(2 * SPAN * g0, 2 * SPAN * g1)
            nc.sync.dma_start(out=w_raw[:, a, cols].bitcast(I32), in_=w4_words[a, :, cols].bitcast(I32))

        def load_scale_rows(plane, rows, j):
            src = rows.rearrange("a (q j) c -> j q a c", j=PACK)[j]
            nc.sync.dma_start(out=plane[j:P:32, :, :].bitcast(I32), in_=src.bitcast(I32))

        def load_r(a):
            src = xr[SPAN * a : SPAN * (a + 1), :].rearrange("(p i) t -> p i t", i=PACK)
            nc.sync.dma_start(out=r_raw[a][:], in_=src)

        def deal_words(g, a):
            raw = w_raw[:, a, 2 * SPAN * g : 2 * SPAN * (g + 1)]
            nc.vector.tensor_copy(
                out=w_dealt[g][a][:].rearrange("p (r m c) -> p r m c", r=PACK, c=2),
                in_=raw.rearrange("p (m r c) -> p r m c", r=PACK, c=2),
            )

        def deal_scales(g, a0, a1):
            raw = ws_early[:, a0:a1, SPAN * g : SPAN * (g + 1)] if g < 2 else ws_late[:, a0:a1, :]
            nc.vector.tensor_copy(
                out=ws_dealt[g][:, a0:a1, :].rearrange("p a (r m) -> p a r m", r=PACK),
                in_=raw.rearrange("p a (m r) -> p a r m", r=PACK),
            )

        def interleaved(dst, src):
            return dst.rearrange("p (c u) i -> p c i u", u=4), src.rearrange("p i (c u) -> p c i u", u=4)

        def round_r(a, cols, copy):
            dst, src = interleaved(r_bf[a][:, cols, :], r_raw[a][:, :, cols])
            copy(out=dst, in_=src)

        def quantise_r(a, h):
            cols = slice(HALF * h, HALF * (h + 1))
            nc.vector.quantize_mx(
                out=r_words[a][:, cols].bitcast(FP8X4),
                scales=r_scales[a][:, cols],
                in_=r_bf[a][:, cols, :].rearrange("p t i -> p (t i)"),
            )

        def multiply(g, r, term, a, cols, start=False, stop=False):
            if start:
                bank = len(acc) % BANKS
                acc[g, r, cols.start] = psum.tile([P, cols.stop - cols.start], F32, name="acc%d" % len(acc), tag="bank%d" % bank)
            if term == "x":
                rhs = x_words[:, a, 2 * cols.start : 2 * cols.stop].bitcast(FP4X4)
                rhs_scale = x_scales[:, a, cols]
            else:
                rhs = r_words[a][:, cols].bitcast(FP8X4)
                rhs_scale = r_scales[a][:, cols]
            nc.tensor.matmul_mx(
                out=acc[g, r, cols.start][:],
                lhsT=w_dealt[g][a][:, 2 * P * r : 2 * P * (r + 1)].bitcast(FP4X4),
                lhsT_scale=ws_dealt[g][:, a, P * r : P * (r + 1)],
                rhs=rhs,
                rhs_scale=rhs_scale,
                start=start,
                stop=stop,
            )

        def activate(g, r, cols):
            nc.scalar.activation(out=y[g][:, r, cols], in_=acc[g, r, cols.start][:], func=SILU, bias=bias[:, g, r : r + 1])

        def store_y(g, r0, r1, cols):
            dst = out_0[SPAN * g : SPAN * (g + 1), :].rearrange("(p r) t -> p r t", r=PACK)
            nc.sync.dma_start(out=dst[:, r0:r1, cols], in_=y[g][:, r0:r1, cols])

        def round_y(g, cols):
            dst, src = interleaved(y_bf[g][:, cols, :], y[g][:, :, cols])
            nc.vector.tensor_copy(out=dst, in_=src)

        def quantise_y(g, cols):
            nc.vector.quantize_mx(
                out=y_words[g][:, cols].bitcast(FP8X4),
                scales=y_scales[:, g, cols],
                in_=y_bf[g][:, cols, :].rearrange("p t r -> p (t r)"),
            )

        def store_words(g, cols):
            dst = out_1[g, :, cols, :].rearrange("p t i -> p (t i)")
            nc.sync.dma_start(out=dst.bitcast(I32), in_=y_words[g][:, cols].bitcast(I32))

        def store_scales(g0, g1, queues):
            for j in range(PACK):
                dst = out_2[g0:g1].rearrange("a (q j) t -> j q a t", j=PACK)[j]
                queues[j].dma_start(out=dst.bitcast(I32), in_=y_scales[j:P:32, g0:g1, :].bitcast(I32))

        whole = slice(0, T)
        quarters = [slice(P * c, P * (c + 1)) for c in range(T // P)]
        halves = [slice(0, HALF), slice(HALF, T)]

        nc.vector.memset(x_scales[:].bitcast(U32), 0)
        nc.vector.memset(ws_early[:].bitcast(U32), 0)
        nc.vector.memset(ws_late[:].bitcast(U32), 0)
        load_w(0, 0, 1)
        for j in range(2):
            load_scale_rows(x_scales, x4_scales, j)
        for j in range(PACK):
            load_scale_rows(ws_early, w4_scales[:, :, 0 : 2 * SPAN], j)
        nc.sync.dma_start(out=x_words[:].bitcast(I32), in_=x4_words.rearrange("a p c -> p a c").bitcast(I32))
        for j in range(2, PACK):
            load_scale_rows(x_scales, x4_scales, j)
        load_w(1, 0, 2)
        load_r(0)
        load_w(0, 1, 2)
        load_r(1)
        nc.sync.dma_start(out=bias[:], in_=b.rearrange("(g p r) -> p g r", g=GROUPS, r=PACK))
        for j in range(PACK):
            load_scale_rows(ws_late, w4_scales[:, :, 2 * SPAN : 3 * SPAN], j)
        load_w(0, 2, 3)
        load_w(1, 2, 3)

        nc.gpsimd.memset(warm_in[:], 0.0)
        nc.scalar.activation(out=warm_out[:], in_=warm_in[:], func=SILU)
        round_r(0, quarters[1], nc.scalar.copy)
        round_r(0, halves[1], nc.scalar.copy)
        round_r(1, slice(SPLIT, T), nc.scalar.copy)
        deal_words(0, 0)
        deal_scales(0, 0, 1)
        deal_words(0, 1)
        deal_scales(0, 1, 2)
        deal_words(1, 1)
        deal_scales(1, 1, 2)
        deal_scales(1, 0, 1)
        round_r(0, quarters[0], nc.vector.tensor_copy)
        deal_words(1, 0)
        quantise_r(0, 0)
        quantise_r(0, 1)
        round_r(1, halves[0], nc.vector.tensor_copy)
        round_r(1, slice(HALF, SPLIT), nc.vector.tensor_copy)
        quantise_r(1, 0)
        quantise_r(1, 1)
        deal_scales(2, 0, 2)
        deal_words(2, 0)
        deal_words(2, 1)

        for r in range(PACK):
            multiply(0, r, "x", 0, whole, start=True)
        for r in range(PACK):
            multiply(0, r, "x", 1, whole)
        for r in range(PACK):
            multiply(1, r, "x", 1, whole, start=True)
        for r in range(PACK - 1):
            multiply(1, r, "x", 0, whole)
        for r in range(PACK):
            multiply(0, r, "r", 0, whole)
        for r in range(PACK):
            multiply(0, r, "r", 1, whole, stop=True)
            activate(0, r, whole)
            store_y(0, r, r + 1, whole)
        round_y(0, whole)
        for r in range(PACK):
            if r == PACK - 1:
                multiply(1, r, "x", 0, whole)
            multiply(1, r, "r", 0, whole)
            multiply(1, r, "r", 1, whole, stop=True)
            activate(1, r, whole)
            if r == 0:
                quantise_y(0, whole)
            if r != 2:
                store_y(1, min(r, 2), r + 1, whole)
            if r == 1:
                store_words(0, whole)
        round_y(1, whole)
        quantise_y(1, whole)
        for r in range(PACK):
            for cols in [whole] if r < PACK - 1 else quarters:
                multiply(2, r, "x", 0, cols, start=True)
                multiply(2, r, "r", 0, cols)
                multiply(2, r, "x", 1, cols)
                multiply(2, r, "r", 1, cols, stop=True)
                activate(2, r, cols)
            if r == 1:
                store_y(2, 0, 2, whole)
                store_words(1, whole)
            elif r == 2:
                store_y(2, 2, 3, whole)
        store_y(2, 3, 4, whole)
        round_y(2, quarters[0])
        round_y(2, quarters[1])
        quantise_y(2, quarters[0])
        round_y(2, quarters[2])
        quantise_y(2, quarters[1])
        store_words(2, halves[0])
        dst, src = interleaved(y_bf[2][:, quarters[3], :], y[2][:, :, quarters[3]])
        nc.scalar.copy(out=dst, in_=src)
        quantise_y(2, quarters[2])
        quantise_y(2, quarters[3])
        store_words(2, halves[1])
        store_scales(0, 3, [nc.scalar, nc.sync, nc.scalar, nc.sync])
